import numpy as np
import ml_dtypes


def mxq(x, axis, fmt="e4m3"):
    dtype, down = {"e4m3": (ml_dtypes.float8_e4m3fn, 7), "e5m2": (ml_dtypes.float8_e5m2, 14)}[fmt]
    v = np.moveaxis(np.asarray(x, np.float32).astype(ml_dtypes.bfloat16).astype(np.float64), axis, -1)
    blocks = v.reshape(v.shape[:-1] + (-1, 32))
    amax = np.abs(blocks).max(-1, keepdims=True)
    byte = np.maximum(np.where(amax > 0, np.frexp(amax)[1] - 1 + 127, 0) - down, 1)
    scale = np.exp2(byte - 127.0)
    codes = (blocks / scale).astype(np.float32).astype(dtype).astype(np.float64)
    return np.moveaxis((codes * scale).reshape(v.shape), -1, axis)


WIDE = False


def mx_kscale(k):
    if not WIDE:
        return np.ones(k)
    levels = np.array([10, -10, 5, -5, 0])
    if k % 512:
        return np.exp2(np.random.permutation(np.resize(levels, k // 32))).repeat(32)
    a = np.empty((k // 512, 16))
    for p in range(k // 512):
        a[p, :8] = np.random.permutation(np.resize(levels, 8))
        for g in range(8):
            far = levels[np.abs(levels - a[p, g]) >= 10]
            a[p, g + 8] = far[np.random.randint(len(far))]
    return np.exp2(a.ravel()).repeat(32)


def f64(x):
    return np.asarray(x).astype(np.float64)


def striped8(idx):
    return np.concatenate([v.reshape(-1, 16).T for v in idx]).astype(np.uint16)


def unstriped8(offs):
    return np.stack([offs[16 * g:16 * g + 16].T.reshape(-1) for g in range(8)]).astype(np.int64)


E2M1 = np.array([0.0, 0.5, 1.0, 1.5, 2.0, 3.0, 4.0, 6.0, -0.0, -0.5, -1.0, -1.5, -2.0, -3.0, -4.0, -6.0])


def pack_weight(w, fmt):
    k, n = w.shape
    w = f64(np.asarray(w, np.float32).astype(ml_dtypes.bfloat16)).reshape(k // 32, 32, n)
    amax = np.abs(w).max(1)
    if fmt == "e4m3":
        byte = np.frexp(amax)[1] - 1 + 127 - 7
    else:
        mant, ex = np.frexp(amax / 6.0)
        byte = np.where(mant > 0.5, ex, ex - 1) + 127
    byte = np.clip(np.where(amax > 0, byte, 1), 1, 254)
    scaled = (w * np.exp2(127.0 - byte)[:, None, :]).reshape(k, n).astype(np.float32)
    by_word = np.ascontiguousarray(scaled.reshape(k // 512, 128, 4, n).transpose(0, 1, 3, 2))
    if fmt == "e4m3":
        words = by_word.astype(ml_dtypes.float8_e4m3fn).view(np.uint8)
    else:
        c = by_word.astype(ml_dtypes.float4_e2m1fn).view(np.uint8) & 0xF
        words = (c[..., 0::2] | (c[..., 1::2] << 4)).reshape(k // 512, 128, 2 * n)
    return np.ascontiguousarray(words), np.ascontiguousarray(byte.astype(np.uint8).reshape(k // 512, 16, n))


def unpack_weight(words, scales, fmt):
    g, _, n = scales.shape
    words = np.ascontiguousarray(words).reshape(g, 128, n, -1)
    if fmt == "e4m3":
        vals = words.view(ml_dtypes.float8_e4m3fn).astype(np.float64)
    else:
        nib = np.empty((g, 128, n, 4), np.uint8)
        nib[..., 0::2] = words & 0xF
        nib[..., 1::2] = words >> 4
        vals = E2M1[nib]
    vals = vals * np.repeat(np.exp2(scales.astype(np.float64) - 127.0), 8, axis=1)[..., None]
    return vals.transpose(0, 1, 3, 2).reshape(g * 512, n)


K, M, T, S = 1024, 1024, 1024, 512


def setup_inputs():
    n = np.random.standard_normal
    s = mx_kscale(K)[:, None]
    u = mx_kscale(512)[:, None]
    p_w4 = pack_weight(n((K, M)) / np.sqrt(K) / s, "e2m1")
    return {
        "xT": (n((K, T)) * s).astype(np.float32),
        "w4_words": p_w4[0],
        "w4_scales": p_w4[1],
        "down": (n((K, 512)) / np.sqrt(K) / s * u.T).astype(np.float32),
        "up": (0.5 * n((512, M)) / np.sqrt(512) / u).astype(np.float32),
        "wgt": np.repeat(np.random.uniform(0.5, 2.0, (8, S)), 16, axis=0).astype(np.float32),
        "wgo": np.repeat(np.random.uniform(0.5, 2.0, (8, S)), 16, axis=0).astype(np.float32),
        "offs": striped8(np.stack([np.random.permutation(T)[:S] for _ in range(8)])),
        "offs2": striped8(np.stack([np.random.permutation(T)[:S] for _ in range(8)])),
    }


def reference(xT, w4_words, w4_scales, down, up, wgt, wgo, offs, offs2):
    idx = unstriped8(offs)
    group = np.arange(K) % 512 // 64
    xg = f64(wgt)[np.arange(K) // 4 % 128] * f64(xT)[np.arange(K)[:, None], idx[group]]
    xT_ = mxq(xg, 0, "e4m3")
    w4_ = unpack_weight(w4_words, w4_scales, "e2m1")
    down_ = mxq(f64(down), 0, "e4m3")
    up_ = mxq(f64(up), 0, "e4m3")
    h_ = mxq(down_.T @ xT_, 0, "e4m3")
    y = w4_.T @ xT_ + up_.T @ h_
    place = unstriped8(offs2)[np.arange(M) % 128 // 16]
    out = np.zeros((M, T))
    out[np.arange(M)[:, None], place] = f64(wgo)[np.arange(M) % 128] * (y)
    return out

@@ -1,0 +1,224 @@
+from contextlib import ExitStack
+
+import concourse.mybir as mybir
+
+K, M, T, S, R = 1024, 1024, 1024, 512, 512
+FLOPS = 2 * S * (K * R + K * M + R * M)
+
+F32 = mybir.dt.float32
+BF16 = mybir.dt.bfloat16
+I32 = mybir.dt.int32
+U32 = mybir.dt.uint32
+U16 = mybir.dt.uint16
+U8 = mybir.dt.uint8
+FP8X4 = mybir.dt.float8_e4m3fn_x4
+FP4X4 = mybir.dt.float4_e2m1fn_x4
+MULT = mybir.AluOpType.mult
+
+P = 128
+PACK = 4
+HALF = S // 2
+QUARTER = S // 4
+CHUNK = 256
+PAGES = 4
+SPLIT_TILES = 2
+
+
+def tile_list_hboth_l_none_kernel(tc, xT, w4_words, w4_scales, down, up, wgt, wgo, offs, offs2, out):
+    nc = tc.nc
+    with ExitStack() as ctx:
+        keep = ctx.enter_context(tc.tile_pool(name="keep", bufs=1))
+        ring = ctx.enter_context(tc.tile_pool(name="ring", bufs=4))
+        psum_h = ctx.enter_context(tc.psum_pool(name="psum_h", bufs=1))
+        psum_y = ctx.enter_context(tc.psum_pool(name="psum_y", bufs=4))
+
+        def held(shape, dtype, name):
+            return keep.tile(shape, dtype, name=name, align_bytes=64)
+
+        pick_list = held([P, S // 16], U16, "pick_list")
+        place_list = held([P, S // 16], U16, "place_list")
+        wgt_sb = held([P, S], F32, "wgt_sb")
+        wgo_sb = held([P, S], F32, "wgo_sb")
+        x_rows = [[held([P, T], F32, "x_rows_%d_%d" % (a, i)) for i in range(PACK)] for a in range(2)]
+        down_raw = [held([P, PACK, R], F32, "down_raw_%d" % a) for a in range(2)]
+        up_raw = [held([P, PACK, CHUNK], F32, "up_raw_%d" % c) for c in range(M // CHUNK)]
+        w4_first = held([P, 2, 2 * CHUNK], U8, "w4_first")
+        w4_rest = held([P, 2, 2 * (M - CHUNK)], U8, "w4_rest")
+        w4_sc = held([P, 2, M], U8, "w4_sc")
+        pages = [held([P, T], F32, "page_%d" % i) for i in range(PAGES)]
+
+        x_view = xT.rearrange("(a p i) t -> a i p t", a=2, i=PACK)
+        down_view = down.rearrange("(a p j) r -> a p j r", a=2, j=PACK)
+        up_view = up.rearrange("(p j) n -> p j n", j=PACK)
+        w4_view = w4_words.bitcast(I32).rearrange("a p n -> p a n")
+
+        nc.gpsimd.memset(w4_sc[:].bitcast(I32), 0)
+        for q in range(4):
+            nc.gpsimd.dma_start(
+                w4_sc[32 * q : 32 * q + 4, :, :].bitcast(I32),
+                w4_scales[:, 4 * q : 4 * q + 4, :].bitcast(I32).rearrange("a r n -> r a n"),
+            )
+        for page in pages:
+            nc.vector.memset(page[:], 0.0)
+
+        nc.sync.dma_start(pick_list[:], offs)
+        nc.sync.dma_start(x_rows[0][0][:], x_view[0, 0])
+        nc.sync.dma_start(wgt_sb[:], wgt)
+        for i in range(1, PACK):
+            nc.sync.dma_start(x_rows[0][i][:], x_view[0, i])
+        nc.sync.dma_start(down_raw[0][:], down_view[0])
+        nc.sync.dma_start(x_rows[1][0][:], x_view[1, 0])
+        nc.sync.dma_start(down_raw[1][:], down_view[1])
+        for i in range(1, PACK):
+            nc.sync.dma_start(x_rows[1][i][:], x_view[1, i])
+        nc.sync.dma_start(up_raw[0][:], up_view[:, :, 0:CHUNK])
+        nc.sync.dma_start(w4_first[:].bitcast(I32), w4_view[:, :, 0 : CHUNK // 2])
+        nc.sync.dma_start(place_list[:], offs2)
+        nc.sync.dma_start(wgo_sb[:], wgo)
+        nc.sync.dma_start(w4_rest[:].bitcast(I32), w4_view[:, :, CHUNK // 2 : M // 2])
+        for c in range(1, M // CHUNK):
+            nc.sync.dma_start(up_raw[c][:], up_view[:, :, c * CHUNK : (c + 1) * CHUNK])
+
+        picked = [held([P, PACK, S], F32, "picked_%d" % a) for a in range(2)]
+        x_codes = [held([P, S], U32, "x_codes_%d" % a) for a in range(2)]
+        x_sc = [held([P, S], U8, "x_sc_%d" % a) for a in range(2)]
+        down_codes = [held([P, R], U32, "down_codes_%d" % a) for a in range(2)]
+        down_sc = [held([P, R], U8, "down_sc_%d" % a) for a in range(2)]
+        up_codes = [held([P, CHUNK], U32, "up_codes_%d" % c) for c in range(M // CHUNK)]
+        up_sc = [held([P, CHUNK], U8, "up_sc_%d" % c) for c in range(M // CHUNK)]
+        h_codes = held([P, S], U32, "h_codes")
+        h_sc = held([P, S], U8, "h_sc")
+        h_banks = [psum_h.tile([P, PACK, QUARTER], F32, name="h_bank_%d" % q) for q in range(4)]
+
+        def gather(a, i, lo, hi):
+            nc.vector.tensor_tensor(
+                picked[a][:, i, lo:hi],
+                x_rows[a][i][:].indirect(pick_list[:, lo // 16 : hi // 16]),
+                wgt_sb[:, lo:hi],
+                MULT,
+            )
+
+        def weave(copy, src, name):
+            width = src.shape[2]
+            woven = held([P, width, PACK], BF16, name)
+            copy(
+                woven[:].rearrange("p (c i) j -> p c j i", i=4),
+                src.rearrange("p j (c i) -> p c j i", i=4),
+            )
+            return woven
+
+        def weave_down(a):
+            woven = held([P, R, PACK], BF16, "down_woven_%d" % a)
+            nc.scalar.copy(
+                woven[:].rearrange("p (t m) j -> p m j t", t=PACK),
+                down_raw[a][:].rearrange("p j (m t) -> p m j t", t=PACK),
+            )
+            return woven
+
+        def quantize(codes, scales, woven):
+            nc.vector.quantize_mx(
+                out=codes.bitcast(FP8X4), scales=scales, in_=woven[:].rearrange("p c j -> p (c j)")
+            )
+
+        def h_passes(a, q):
+            cols = slice(q * QUARTER, (q + 1) * QUARTER)
+            for t in range(PACK):
+                rows = slice(t * P, (t + 1) * P)
+                nc.tensor.matmul_mx(
+                    out=h_banks[q][:, t, :],
+                    lhsT=down_codes[a][:, rows].bitcast(FP8X4),
+                    lhsT_scale=down_sc[a][:, rows],
+                    rhs=x_codes[a][:, cols].bitcast(FP8X4),
+                    rhs_scale=x_sc[a][:, cols],
+                    start=(a == 0 and t == 0),
+                    stop=(a == 1 and t == PACK - 1),
+                )
+
+        def h_weave(half):
+            woven = held([P, HALF, PACK], BF16, "h_woven_%d" % half)
+            for u in range(2):
+                nc.scalar.copy(
+                    woven[:, u * QUARTER : (u + 1) * QUARTER, :],
+                    h_banks[2 * half + u][:].rearrange("p t s -> p s t"),
+                )
+            return woven
+
+        def y_base(n, lo, hi):
+            bank = psum_y.tile([P, S], F32, name="y_bank")
+            words, first = (w4_first, 0) if n * P < CHUNK else (w4_rest, CHUNK)
+            step = S if hi - lo == S else QUARTER
+            for a in range(2):
+                for s0 in range(lo, hi, step):
+                    nc.tensor.matmul_mx(
+                        out=bank[:, s0 - lo : s0 - lo + step],
+                        lhsT=words[:, a, 2 * (n * P - first) : 2 * (n * P - first + P)].bitcast(FP4X4),
+                        lhsT_scale=w4_sc[:, a, n * P : (n + 1) * P],
+                        rhs=x_codes[a][:, s0 : s0 + step].bitcast(FP8X4),
+                        rhs_scale=x_sc[a][:, s0 : s0 + step],
+                        start=(a == 0 and s0 == lo),
+                        stop=False,
+                    )
+            return bank
+
+        def y_finish(n, lo, hi, bank):
+            c, n0 = divmod(n * P, CHUNK)
+            nc.tensor.matmul_mx(
+                out=bank[:, 0 : hi - lo],
+                lhsT=up_codes[c][:, n0 : n0 + P].bitcast(FP8X4),
+                lhsT_scale=up_sc[c][:, n0 : n0 + P],
+                rhs=h_codes[:, lo:hi].bitcast(FP8X4),
+                rhs_scale=h_sc[:, lo:hi],
+                start=False,
+                stop=True,
+            )
+            y_sb = ring.tile([P, S], F32, name="y_sb")
+            nc.scalar.copy(y_sb[:, 0 : hi - lo], bank[:, 0 : hi - lo])
+            nc.vector.tensor_tensor(
+                pages[n % PAGES][:].indirect(place_list[:, lo // 16 : hi // 16]),
+                y_sb[:, 0 : hi - lo],
+                wgo_sb[:, lo:hi],
+                MULT,
+            )
+            if hi == S:
+                nc.sync.dma_start(out[n * P : (n + 1) * P, :], pages[n % PAGES][:])
+
+        for i in range(PACK):
+            gather(0, i, 0, S)
+        x0 = weave(nc.vector.tensor_copy, picked[0][:], "x_woven_0")
+        d0 = weave_down(0)
+        quantize(x_codes[0][:], x_sc[0][:], x0)
+        gather(1, 0, 0, S)
+        quantize(down_codes[0][:], down_sc[0][:], d0)
+        for q in range(4):
+            h_passes(0, q)
+        d1 = weave_down(1)
+        gather(1, 1, 0, S)
+        gather(1, 2, 0, HALF)
+        quantize(down_codes[1][:], down_sc[1][:], d1)
+        gather(1, 3, 0, HALF)
+        xa = weave(nc.vector.tensor_copy, picked[1][:, :, 0:HALF], "x_woven_1a")
+        u0 = weave(nc.scalar.copy, up_raw[0][:], "up_woven_0")
+        gather(1, 2, HALF, S)
+        quantize(x_codes[1][:, 0:HALF], x_sc[1][:, 0:HALF], xa)
+        h_passes(1, 0)
+        h_passes(1, 1)
+        ha = h_weave(0)
+        banks_a = [y_base(n, 0, HALF) for n in range(SPLIT_TILES)]
+        gather(1, 3, HALF, S)
+        quantize(up_codes[0][:], up_sc[0][:], u0)
+        xb = weave(nc.vector.tensor_copy, picked[1][:, :, HALF:S], "x_woven_1b")
+        quantize(h_codes[:, 0:HALF], h_sc[:, 0:HALF], ha)
+        quantize(x_codes[1][:, HALF:S], x_sc[1][:, HALF:S], xb)
+        y_finish(0, 0, HALF, banks_a[0])
+        h_passes(1, 2)
+        h_passes(1, 3)
+        hb = h_weave(1)
+        quantize(h_codes[:, HALF:S], h_sc[:, HALF:S], hb)
+        y_finish(1, 0, HALF, banks_a[1])
+        for n in range(SPLIT_TILES):
+            y_finish(n, HALF, S, y_base(n, HALF, S))
+        for n in range(SPLIT_TILES, M // P):
+            c, n0 = divmod(n * P, CHUNK)
+            if n0 == 0:
+                quantize(up_codes[c][:], up_sc[c][:], weave(nc.scalar.copy, up_raw[c][:], "up_woven_%d" % c))
+            y_finish(n, 0, S, y_base(n, 0, S))

@@ -17,107 +17,121 @@ MULT = mybir.AluOpType.mult
 
 P = 128
 PACK = 4
+PASSES = K // (P * PACK)
+GROUP = 16
 HALF = S // 2
 QUARTER = S // 4
-CHUNK = 256
-PAGES = 4
 SPLIT_TILES = 2
+FIRST_COLS = SPLIT_TILES * P
+UP_CHUNKS = ((0, FIRST_COLS), (FIRST_COLS, 2 * FIRST_COLS), (2 * FIRST_COLS, M))
+LAST_CHUNK_BEFORE = 3
+PAGES = 3
+Y_BANKS = 2
+Y_COPIES = 4
 
 
 def tile_list_hboth_l_none_kernel(tc, xT, w4_words, w4_scales, down, up, wgt, wgo, offs, offs2, out):
     nc = tc.nc
     with ExitStack() as ctx:
         keep = ctx.enter_context(tc.tile_pool(name="keep", bufs=1))
-        ring = ctx.enter_context(tc.tile_pool(name="ring", bufs=4))
+        ring = ctx.enter_context(tc.tile_pool(name="ring", bufs=Y_COPIES))
         psum_h = ctx.enter_context(tc.psum_pool(name="psum_h", bufs=1))
-        psum_y = ctx.enter_context(tc.psum_pool(name="psum_y", bufs=4))
+        psum_y = ctx.enter_context(tc.psum_pool(name="psum_y", bufs=Y_BANKS))
 
-        def held(shape, dtype, name):
-            return keep.tile(shape, dtype, name=name, align_bytes=64)
+        def held(shape, dtype, name, tag=None):
+            return keep.tile(shape, dtype, name=name, tag=tag or name, align_bytes=64)
 
-        pick_list = held([P, S // 16], U16, "pick_list")
-        place_list = held([P, S // 16], U16, "place_list")
+        pick_list = held([P, S // GROUP], U16, "pick_list")
+        place_list = held([P, S // GROUP], U16, "place_list")
         wgt_sb = held([P, S], F32, "wgt_sb")
-        wgo_sb = held([P, S], F32, "wgo_sb")
-        x_rows = [[held([P, T], F32, "x_rows_%d_%d" % (a, i)) for i in range(PACK)] for a in range(2)]
-        down_raw = [held([P, PACK, R], F32, "down_raw_%d" % a) for a in range(2)]
-        up_raw = [held([P, PACK, CHUNK], F32, "up_raw_%d" % c) for c in range(M // CHUNK)]
-        w4_first = held([P, 2, 2 * CHUNK], U8, "w4_first")
-        w4_rest = held([P, 2, 2 * (M - CHUNK)], U8, "w4_rest")
-        w4_sc = held([P, 2, M], U8, "w4_sc")
+        x_rows = [[held([P, T], F32, "x_rows_%d_%d" % (a, i)) for i in range(PACK)] for a in range(PASSES)]
+        down_raw = [held([P, PACK, R], F32, "down_raw_%d" % a) for a in range(PASSES)]
+        w4_first = held([P, PASSES, 2 * FIRST_COLS], U8, "w4_first")
+        w4_sc = held([P, PASSES, M], U8, "w4_sc")
         pages = [held([P, T], F32, "page_%d" % i) for i in range(PAGES)]
 
-        x_view = xT.rearrange("(a p i) t -> a i p t", a=2, i=PACK)
-        down_view = down.rearrange("(a p j) r -> a p j r", a=2, j=PACK)
-        up_view = up.rearrange("(p j) n -> p j n", j=PACK)
+        x_view = xT.rearrange("(a p i) t -> a i p t", a=PASSES, i=PACK)
+        down_view = down.rearrange("(a p i) r -> a p i r", a=PASSES, i=PACK)
+        up_view = up.rearrange("(u t e) n -> e u t n", t=PACK, e=2)
         w4_view = w4_words.bitcast(I32).rearrange("a p n -> p a n")
 
         nc.gpsimd.memset(w4_sc[:].bitcast(I32), 0)
-        for q in range(4):
-            nc.gpsimd.dma_start(
-                w4_sc[32 * q : 32 * q + 4, :, :].bitcast(I32),
-                w4_scales[:, 4 * q : 4 * q + 4, :].bitcast(I32).rearrange("a r n -> r a n"),
-            )
         for page in pages:
             nc.vector.memset(page[:], 0.0)
+
+        def load_up(c, tag):
+            lo, hi = UP_CHUNKS[c]
+            raw = held([P, PACK, hi - lo], F32, "up_raw_%d" % c, tag)
+            for e in range(2):
+                nc.sync.dma_start(raw[e:P:2, :, :], up_view[e][:, :, lo:hi])
+            return raw
 
         nc.sync.dma_start(pick_list[:], offs)
         nc.sync.dma_start(x_rows[0][0][:], x_view[0, 0])
         nc.sync.dma_start(wgt_sb[:], wgt)
+        nc.sync.dma_start(place_list[:], offs2)
         for i in range(1, PACK):
             nc.sync.dma_start(x_rows[0][i][:], x_view[0, i])
         nc.sync.dma_start(down_raw[0][:], down_view[0])
-        nc.sync.dma_start(x_rows[1][0][:], x_view[1, 0])
-        nc.sync.dma_start(down_raw[1][:], down_view[1])
-        for i in range(1, PACK):
+        for i in range(2):
             nc.sync.dma_start(x_rows[1][i][:], x_view[1, i])
-        nc.sync.dma_start(up_raw[0][:], up_view[:, :, 0:CHUNK])
-        nc.sync.dma_start(w4_first[:].bitcast(I32), w4_view[:, :, 0 : CHUNK // 2])
-        nc.sync.dma_start(place_list[:], offs2)
+        nc.sync.dma_start(down_raw[1][:], down_view[1])
+        for i in range(2, PACK):
+            nc.sync.dma_start(x_rows[1][i][:], x_view[1, i])
+        up_raw = [load_up(0, None)]
+        nc.sync.dma_start(w4_first[:].bitcast(I32), w4_view[:, :, 0 : FIRST_COLS // 2])
+        for q in range(4):
+            nc.sync.dma_start(
+                w4_sc[32 * q : 32 * q + 4, :, :].bitcast(I32),
+                w4_scales[:, 4 * q : 4 * q + 4, :].bitcast(I32).rearrange("a s n -> s a n"),
+            )
+        wgo_sb = held([P, S], F32, "wgo_sb")
         nc.sync.dma_start(wgo_sb[:], wgo)
-        nc.sync.dma_start(w4_rest[:].bitcast(I32), w4_view[:, :, CHUNK // 2 : M // 2])
-        for c in range(1, M // CHUNK):
-            nc.sync.dma_start(up_raw[c][:], up_view[:, :, c * CHUNK : (c + 1) * CHUNK])
 
-        picked = [held([P, PACK, S], F32, "picked_%d" % a) for a in range(2)]
-        x_codes = [held([P, S], U32, "x_codes_%d" % a) for a in range(2)]
-        x_sc = [held([P, S], U8, "x_sc_%d" % a) for a in range(2)]
-        down_codes = [held([P, R], U32, "down_codes_%d" % a) for a in range(2)]
-        down_sc = [held([P, R], U8, "down_sc_%d" % a) for a in range(2)]
-        up_codes = [held([P, CHUNK], U32, "up_codes_%d" % c) for c in range(M // CHUNK)]
-        up_sc = [held([P, CHUNK], U8, "up_sc_%d" % c) for c in range(M // CHUNK)]
+        picked_0 = held([P, PACK, S], F32, "picked_0")
+        picked_1 = held([P, PACK + 2, HALF], F32, "picked_1")
+        picked_first = picked_1[:, 2 : PACK + 2, :]
+        picked_second = picked_1[:, 0:PACK, :]
+        x_codes = [held([P, S], U32, "x_codes_%d" % a) for a in range(PASSES)]
+        x_sc = [held([P, S], U8, "x_sc_%d" % a) for a in range(PASSES)]
+        down_codes = [held([P, R], U32, "down_codes_%d" % a) for a in range(PASSES)]
+        down_sc = [held([P, R], U8, "down_sc_%d" % a) for a in range(PASSES)]
+        up_codes = [held([P, hi - lo], U32, "up_codes_%d" % lo) for lo, hi in UP_CHUNKS]
+        up_sc = [held([P, hi - lo], U8, "up_sc_%d" % lo) for lo, hi in UP_CHUNKS]
         h_codes = held([P, S], U32, "h_codes")
         h_sc = held([P, S], U8, "h_sc")
-        h_banks = [psum_h.tile([P, PACK, QUARTER], F32, name="h_bank_%d" % q) for q in range(4)]
+        h_banks = [psum_h.tile([P, PACK, QUARTER], F32, name="h_bank_%d" % q, tag="h_bank_%d" % q) for q in range(4)]
 
-        def gather(a, i, lo, hi):
+        def gather(a, i, lo, hi, dst):
             nc.vector.tensor_tensor(
-                picked[a][:, i, lo:hi],
-                x_rows[a][i][:].indirect(pick_list[:, lo // 16 : hi // 16]),
+                dst,
+                x_rows[a][i][:].indirect(pick_list[:, lo // GROUP : hi // GROUP]),
                 wgt_sb[:, lo:hi],
                 MULT,
             )
 
-        def weave(copy, src, name):
-            width = src.shape[2]
-            woven = held([P, width, PACK], BF16, name)
+        def weave_into(copy, woven, src):
             copy(
-                woven[:].rearrange("p (c i) j -> p c j i", i=4),
-                src.rearrange("p j (c i) -> p c j i", i=4),
+                woven.rearrange("p (c d) i -> p c i d", d=4),
+                src.rearrange("p i (c d) -> p c i d", d=4),
             )
+
+        def weave(copy, src, name):
+            woven = held([P, src.shape[2], PACK], BF16, name)
+            weave_into(copy, woven[:], src)
             return woven
 
-        def weave_down(a):
-            woven = held([P, R, PACK], BF16, "down_woven_%d" % a)
-            nc.scalar.copy(
-                woven[:].rearrange("p (t m) j -> p m j t", t=PACK),
-                down_raw[a][:].rearrange("p j (m t) -> p m j t", t=PACK),
+        def weave_down(copy, a, lo, hi):
+            woven = held([P, (hi - lo) * P, PACK], BF16, "down_woven_%d_%d" % (a, lo))
+            copy(
+                woven[:].rearrange("p (t u e) i -> p t u i e", t=hi - lo, e=2),
+                down_raw[a][:].rearrange("p i (u t e) -> p t u i e", t=PACK, e=2)[:, lo:hi],
             )
             return woven
 
         def quantize(codes, scales, woven):
             nc.vector.quantize_mx(
-                out=codes.bitcast(FP8X4), scales=scales, in_=woven[:].rearrange("p c j -> p (c j)")
+                out=codes.bitcast(FP8X4), scales=scales, in_=woven[:, :, :].rearrange("p c i -> p (c i)")
             )
 
         def h_passes(a, q):
@@ -131,23 +145,24 @@ def tile_list_hboth_l_none_kernel(tc, xT, w4_words, w4_scales, down, up, wgt, wg
                     rhs=x_codes[a][:, cols].bitcast(FP8X4),
                     rhs_scale=x_sc[a][:, cols],
                     start=(a == 0 and t == 0),
-                    stop=(a == 1 and t == PACK - 1),
+                    stop=(a == PASSES - 1 and t == PACK - 1),
                 )
 
-        def h_weave(half):
-            woven = held([P, HALF, PACK], BF16, "h_woven_%d" % half)
-            for u in range(2):
+        def h_weave(half, tag=None):
+            woven = held([P, HALF, PACK], BF16, "h_woven_%d" % half, tag)
+            for q in range(2):
                 nc.scalar.copy(
-                    woven[:, u * QUARTER : (u + 1) * QUARTER, :],
-                    h_banks[2 * half + u][:].rearrange("p t s -> p s t"),
+                    woven[:, q * QUARTER : (q + 1) * QUARTER, :],
+                    h_banks[2 * half + q][:].rearrange("p t s -> p s t"),
                 )
             return woven
 
-        def y_base(n, lo, hi):
-            bank = psum_y.tile([P, S], F32, name="y_bank")
-            words, first = (w4_first, 0) if n * P < CHUNK else (w4_rest, CHUNK)
+        def y_base(n, lo, hi, bank=None):
+            if bank is None:
+                bank = psum_y.tile([P, S], F32, name="y_bank")
+            words, first = (w4_first, 0) if n < SPLIT_TILES else (w4_rest, FIRST_COLS)
             step = S if hi - lo == S else QUARTER
-            for a in range(2):
+            for a in (1, 0):
                 for s0 in range(lo, hi, step):
                     nc.tensor.matmul_mx(
                         out=bank[:, s0 - lo : s0 - lo + step],
@@ -155,13 +170,14 @@ def tile_list_hboth_l_none_kernel(tc, xT, w4_words, w4_scales, down, up, wgt, wg
                         lhsT_scale=w4_sc[:, a, n * P : (n + 1) * P],
                         rhs=x_codes[a][:, s0 : s0 + step].bitcast(FP8X4),
                         rhs_scale=x_sc[a][:, s0 : s0 + step],
-                        start=(a == 0 and s0 == lo),
+                        start=(a == 1 and s0 == lo),
                         stop=False,
                     )
             return bank
 
-        def y_finish(n, lo, hi, bank):
-            c, n0 = divmod(n * P, CHUNK)
+        def y_finish(n, lo, hi, bank, y_sb=None):
+            c = max(i for i, chunk in enumerate(UP_CHUNKS) if chunk[0] <= n * P)
+            n0 = n * P - UP_CHUNKS[c][0]
             nc.tensor.matmul_mx(
                 out=bank[:, 0 : hi - lo],
                 lhsT=up_codes[c][:, n0 : n0 + P].bitcast(FP8X4),
@@ -171,10 +187,11 @@ def tile_list_hboth_l_none_kernel(tc, xT, w4_words, w4_scales, down, up, wgt, wg
                 start=False,
                 stop=True,
             )
-            y_sb = ring.tile([P, S], F32, name="y_sb")
+            if y_sb is None:
+                y_sb = ring.tile([P, S], F32, name="y_sb")
             nc.scalar.copy(y_sb[:, 0 : hi - lo], bank[:, 0 : hi - lo])
             nc.vector.tensor_tensor(
-                pages[n % PAGES][:].indirect(place_list[:, lo // 16 : hi // 16]),
+                pages[n % PAGES][:].indirect(place_list[:, lo // GROUP : hi // GROUP]),
                 y_sb[:, 0 : hi - lo],
                 wgo_sb[:, lo:hi],
                 MULT,
@@ -182,43 +199,64 @@ def tile_list_hboth_l_none_kernel(tc, xT, w4_words, w4_scales, down, up, wgt, wg
             if hi == S:
                 nc.sync.dma_start(out[n * P : (n + 1) * P, :], pages[n % PAGES][:])
 
+        up_tags = [None, "picked_0", "down_raw_0"]
         for i in range(PACK):
-            gather(0, i, 0, S)
-        x0 = weave(nc.vector.tensor_copy, picked[0][:], "x_woven_0")
-        d0 = weave_down(0)
-        quantize(x_codes[0][:], x_sc[0][:], x0)
-        gather(1, 0, 0, S)
-        quantize(down_codes[0][:], down_sc[0][:], d0)
+            gather(0, i, 0, S, picked_0[:, i, :])
+        x_woven_0 = weave(nc.vector.tensor_copy, picked_0[:], "x_woven_0")
+        up_raw.append(load_up(1, up_tags[1]))
+        quantize(x_codes[0][:], x_sc[0][:], x_woven_0)
+        down_woven_0 = weave_down(nc.scalar.copy, 0, 0, PACK)
+        up_raw.append(load_up(2, up_tags[2]))
+        quantize(down_codes[0][:], down_sc[0][:], down_woven_0)
+        w4_rest = held([P, PASSES, 2 * (M - FIRST_COLS)], U8, "w4_rest", "down_woven_0_0")
+        nc.sync.dma_start(w4_rest[:].bitcast(I32), w4_view[:, :, FIRST_COLS // 2 : M // 2])
         for q in range(4):
             h_passes(0, q)
-        d1 = weave_down(1)
-        gather(1, 1, 0, S)
-        gather(1, 2, 0, HALF)
-        quantize(down_codes[1][:], down_sc[1][:], d1)
-        gather(1, 3, 0, HALF)
-        xa = weave(nc.vector.tensor_copy, picked[1][:, :, 0:HALF], "x_woven_1a")
-        u0 = weave(nc.scalar.copy, up_raw[0][:], "up_woven_0")
-        gather(1, 2, HALF, S)
-        quantize(x_codes[1][:, 0:HALF], x_sc[1][:, 0:HALF], xa)
-        h_passes(1, 0)
-        h_passes(1, 1)
-        ha = h_weave(0)
-        banks_a = [y_base(n, 0, HALF) for n in range(SPLIT_TILES)]
-        gather(1, 3, HALF, S)
-        quantize(up_codes[0][:], up_sc[0][:], u0)
-        xb = weave(nc.vector.tensor_copy, picked[1][:, :, HALF:S], "x_woven_1b")
-        quantize(h_codes[:, 0:HALF], h_sc[:, 0:HALF], ha)
-        quantize(x_codes[1][:, HALF:S], x_sc[1][:, HALF:S], xb)
-        y_finish(0, 0, HALF, banks_a[0])
-        h_passes(1, 2)
-        h_passes(1, 3)
-        hb = h_weave(1)
-        quantize(h_codes[:, HALF:S], h_sc[:, HALF:S], hb)
-        y_finish(1, 0, HALF, banks_a[1])
-        for n in range(SPLIT_TILES):
-            y_finish(n, HALF, S, y_base(n, HALF, S))
+
+        for i in range(2):
+            gather(1, i, 0, HALF, picked_first[:, i, :])
+            gather(1, i, HALF, S, picked_second[:, i, :])
+        for copy, lo in ((nc.vector.tensor_copy, 0), (nc.scalar.copy, 2)):
+            cols = slice(lo * P, (lo + 2) * P)
+            quantize(down_codes[1][:, cols], down_sc[1][:, cols], weave_down(copy, 1, lo, lo + 2))
+
+        gather(1, 2, 0, HALF, picked_first[:, 2, :])
+        quarters = [slice(q * QUARTER, (q + 1) * QUARTER) for q in range(2)]
+        for cols in quarters:
+            gather(1, 3, cols.start, cols.stop, picked_first[:, 3, cols])
+        x_woven_first = [
+            weave(nc.vector.tensor_copy, picked_first[:, :, cols], "x_woven_first_%d" % q)
+            for q, cols in enumerate(quarters)
+        ]
+        up_woven_0 = weave(nc.scalar.copy, up_raw[0][:], "up_woven_0")
+        for q, cols in enumerate(quarters):
+            quantize(x_codes[1][:, cols], x_sc[1][:, cols], x_woven_first[q])
+            h_passes(1, q)
+        h_woven_first = h_weave(0, "up_raw_0")
+        bank_0_first = y_base(0, 0, HALF)
+
+        gather(1, 2, HALF, S, picked_second[:, 2, :])
+        gather(1, 3, HALF, S, picked_second[:, 3, :])
+        quantize(up_codes[0][:], up_sc[0][:], up_woven_0)
+        quantize(h_codes[:, 0:HALF], h_sc[:, 0:HALF], h_woven_first)
+        x_woven_second = held([P, HALF, PACK], BF16, "x_woven_second", "up_raw_0")
+        for cols in quarters:
+            weave_into(nc.vector.tensor_copy, x_woven_second[:, cols, :], picked_second[:, :, cols])
+        for q, cols in enumerate(quarters):
+            tokens = slice(HALF + cols.start, HALF + cols.stop)
+            quantize(x_codes[1][:, tokens], x_sc[1][:, tokens], x_woven_second[:, cols, :])
+            h_passes(1, 2 + q)
+        y_finish(0, 0, HALF, bank_0_first)
+        h_woven_second = h_weave(1)
+        quantize(h_codes[:, HALF:S], h_sc[:, HALF:S], h_woven_second)
+        y_finish(1, 0, HALF, y_base(1, 0, HALF, psum_h.tile([P, S], F32, name="y_bank_1_first", tag="h_bank_2")))
+
+        def up_chunk(c, width):
+            quantize(up_codes[c][:], up_sc[c][:], weave(nc.scalar.copy, up_raw[c][:], "up_woven_%d" % c))
+            return held([P, width], F32, "y_sb_after_up_%d" % c, up_tags[c])
+
+        y_finish(0, HALF, S, y_base(0, HALF, S))
+        y_finish(1, HALF, S, y_base(1, HALF, S), up_chunk(1, HALF))
         for n in range(SPLIT_TILES, M // P):
-            c, n0 = divmod(n * P, CHUNK)
-            if n0 == 0:
-                quantize(up_codes[c][:], up_sc[c][:], weave(nc.scalar.copy, up_raw[c][:], "up_woven_%d" % c))
-            y_finish(n, 0, S, y_base(n, 0, S))
+            y_sb = up_chunk(2, S) if n == LAST_CHUNK_BEFORE else None
+            y_finish(n, 0, S, y_base(n, 0, S), y_sb)

from contextlib import ExitStack

import concourse.mybir as mybir

K, M, T, S, R = 1024, 1024, 1024, 512, 512
FLOPS = 2 * S * (K * R + K * M + R * M)

F32 = mybir.dt.float32
BF16 = mybir.dt.bfloat16
I32 = mybir.dt.int32
U32 = mybir.dt.uint32
U16 = mybir.dt.uint16
U8 = mybir.dt.uint8
FP8X4 = mybir.dt.float8_e4m3fn_x4
FP4X4 = mybir.dt.float4_e2m1fn_x4
MULT = mybir.AluOpType.mult

P = 128
PACK = 4
PASSES = K // (P * PACK)
GROUP = 16
HALF = S // 2
QUARTER = S // 4
SPLIT_TILES = 2
FIRST_COLS = SPLIT_TILES * P
UP_CHUNKS = ((0, FIRST_COLS), (FIRST_COLS, 2 * FIRST_COLS), (2 * FIRST_COLS, M))
LAST_CHUNK_BEFORE = 3
PAGES = 3
Y_BANKS = 2
Y_COPIES = 4


def tile_list_hboth_l_none_kernel(tc, xT, w4_words, w4_scales, down, up, wgt, wgo, offs, offs2, out):
    nc = tc.nc
    with ExitStack() as ctx:
        keep = ctx.enter_context(tc.tile_pool(name="keep", bufs=1))
        ring = ctx.enter_context(tc.tile_pool(name="ring", bufs=Y_COPIES))
        psum_h = ctx.enter_context(tc.psum_pool(name="psum_h", bufs=1))
        psum_y = ctx.enter_context(tc.psum_pool(name="psum_y", bufs=Y_BANKS))

        def held(shape, dtype, name, tag=None):
            return keep.tile(shape, dtype, name=name, tag=tag or name, align_bytes=64)

        pick_list = held([P, S // GROUP], U16, "pick_list")
        place_list = held([P, S // GROUP], U16, "place_list")
        wgt_sb = held([P, S], F32, "wgt_sb")
        x_rows = [[held([P, T], F32, "x_rows_%d_%d" % (a, i)) for i in range(PACK)] for a in range(PASSES)]
        down_raw = [held([P, PACK, R], F32, "down_raw_%d" % a) for a in range(PASSES)]
        w4_first = held([P, PASSES, 2 * FIRST_COLS], U8, "w4_first")
        w4_sc = held([P, PASSES, M], U8, "w4_sc")
        pages = [held([P, T], F32, "page_%d" % i) for i in range(PAGES)]

        x_view = xT.rearrange("(a p i) t -> a i p t", a=PASSES, i=PACK)
        down_view = down.rearrange("(a p i) r -> a p i r", a=PASSES, i=PACK)
        up_view = up.rearrange("(u t e) n -> e u t n", t=PACK, e=2)
        w4_view = w4_words.bitcast(I32).rearrange("a p n -> p a n")

        nc.gpsimd.memset(w4_sc[:].bitcast(I32), 0)
        for page in pages:
            nc.vector.memset(page[:], 0.0)

        def load_up(c, tag):
            lo, hi = UP_CHUNKS[c]
            raw = held([P, PACK, hi - lo], F32, "up_raw_%d" % c, tag)
            for e in range(2):
                nc.sync.dma_start(raw[e:P:2, :, :], up_view[e][:, :, lo:hi])
            return raw

        nc.sync.dma_start(pick_list[:], offs)
        nc.sync.dma_start(x_rows[0][0][:], x_view[0, 0])
        nc.sync.dma_start(wgt_sb[:], wgt)
        nc.sync.dma_start(place_list[:], offs2)
        for i in range(1, PACK):
            nc.sync.dma_start(x_rows[0][i][:], x_view[0, i])
        nc.sync.dma_start(down_raw[0][:], down_view[0])
        for i in range(2):
            nc.sync.dma_start(x_rows[1][i][:], x_view[1, i])
        nc.sync.dma_start(down_raw[1][:], down_view[1])
        for i in range(2, PACK):
            nc.sync.dma_start(x_rows[1][i][:], x_view[1, i])
        up_raw = [load_up(0, None)]
        nc.sync.dma_start(w4_first[:].bitcast(I32), w4_view[:, :, 0 : FIRST_COLS // 2])
        for q in range(4):
            nc.sync.dma_start(
                w4_sc[32 * q : 32 * q + 4, :, :].bitcast(I32),
                w4_scales[:, 4 * q : 4 * q + 4, :].bitcast(I32).rearrange("a s n -> s a n"),
            )
        wgo_sb = held([P, S], F32, "wgo_sb")
        nc.sync.dma_start(wgo_sb[:], wgo)

        picked_0 = held([P, PACK, S], F32, "picked_0")
        picked_1 = held([P, PACK + 2, HALF], F32, "picked_1")
        picked_first = picked_1[:, 2 : PACK + 2, :]
        picked_second = picked_1[:, 0:PACK, :]
        x_codes = [held([P, S], U32, "x_codes_%d" % a) for a in range(PASSES)]
        x_sc = [held([P, S], U8, "x_sc_%d" % a) for a in range(PASSES)]
        down_codes = [held([P, R], U32, "down_codes_%d" % a) for a in range(PASSES)]
        down_sc = [held([P, R], U8, "down_sc_%d" % a) for a in range(PASSES)]
        up_codes = [held([P, hi - lo], U32, "up_codes_%d" % lo) for lo, hi in UP_CHUNKS]
        up_sc = [held([P, hi - lo], U8, "up_sc_%d" % lo) for lo, hi in UP_CHUNKS]
        h_codes = held([P, S], U32, "h_codes")
        h_sc = held([P, S], U8, "h_sc")
        h_banks = [psum_h.tile([P, PACK, QUARTER], F32, name="h_bank_%d" % q, tag="h_bank_%d" % q) for q in range(4)]

        def gather(a, i, lo, hi, dst):
            nc.vector.tensor_tensor(
                dst,
                x_rows[a][i][:].indirect(pick_list[:, lo // GROUP : hi // GROUP]),
                wgt_sb[:, lo:hi],
                MULT,
            )

        def weave_into(copy, woven, src):
            copy(
                woven.rearrange("p (c d) i -> p c i d", d=4),
                src.rearrange("p i (c d) -> p c i d", d=4),
            )

        def weave(copy, src, name):
            woven = held([P, src.shape[2], PACK], BF16, name)
            weave_into(copy, woven[:], src)
            return woven

        def weave_down(copy, a, lo, hi):
            woven = held([P, (hi - lo) * P, PACK], BF16, "down_woven_%d_%d" % (a, lo))
            copy(
                woven[:].rearrange("p (t u e) i -> p t u i e", t=hi - lo, e=2),
                down_raw[a][:].rearrange("p i (u t e) -> p t u i e", t=PACK, e=2)[:, lo:hi],
            )
            return woven

        def quantize(codes, scales, woven):
            nc.vector.quantize_mx(
                out=codes.bitcast(FP8X4), scales=scales, in_=woven[:, :, :].rearrange("p c i -> p (c i)")
            )

        def h_passes(a, q):
            cols = slice(q * QUARTER, (q + 1) * QUARTER)
            for t in range(PACK):
                rows = slice(t * P, (t + 1) * P)
                nc.tensor.matmul_mx(
                    out=h_banks[q][:, t, :],
                    lhsT=down_codes[a][:, rows].bitcast(FP8X4),
                    lhsT_scale=down_sc[a][:, rows],
                    rhs=x_codes[a][:, cols].bitcast(FP8X4),
                    rhs_scale=x_sc[a][:, cols],
                    start=(a == 0 and t == 0),
                    stop=(a == PASSES - 1 and t == PACK - 1),
                )

        def h_weave(half, tag=None):
            woven = held([P, HALF, PACK], BF16, "h_woven_%d" % half, tag)
            for q in range(2):
                nc.scalar.copy(
                    woven[:, q * QUARTER : (q + 1) * QUARTER, :],
                    h_banks[2 * half + q][:].rearrange("p t s -> p s t"),
                )
            return woven

        def y_base(n, lo, hi, bank=None):
            if bank is None:
                bank = psum_y.tile([P, S], F32, name="y_bank")
            words, first = (w4_first, 0) if n < SPLIT_TILES else (w4_rest, FIRST_COLS)
            step = S if hi - lo == S else QUARTER
            for a in (1, 0):
                for s0 in range(lo, hi, step):
                    nc.tensor.matmul_mx(
                        out=bank[:, s0 - lo : s0 - lo + step],
                        lhsT=words[:, a, 2 * (n * P - first) : 2 * (n * P - first + P)].bitcast(FP4X4),
                        lhsT_scale=w4_sc[:, a, n * P : (n + 1) * P],
                        rhs=x_codes[a][:, s0 : s0 + step].bitcast(FP8X4),
                        rhs_scale=x_sc[a][:, s0 : s0 + step],
                        start=(a == 1 and s0 == lo),
                        stop=False,
                    )
            return bank

        def y_finish(n, lo, hi, bank, y_sb=None):
            c = max(i for i, chunk in enumerate(UP_CHUNKS) if chunk[0] <= n * P)
            n0 = n * P - UP_CHUNKS[c][0]
            nc.tensor.matmul_mx(
                out=bank[:, 0 : hi - lo],
                lhsT=up_codes[c][:, n0 : n0 + P].bitcast(FP8X4),
                lhsT_scale=up_sc[c][:, n0 : n0 + P],
                rhs=h_codes[:, lo:hi].bitcast(FP8X4),
                rhs_scale=h_sc[:, lo:hi],
                start=False,
                stop=True,
            )
            if y_sb is None:
                y_sb = ring.tile([P, S], F32, name="y_sb")
            nc.scalar.copy(y_sb[:, 0 : hi - lo], bank[:, 0 : hi - lo])
            nc.vector.tensor_tensor(
                pages[n % PAGES][:].indirect(place_list[:, lo // GROUP : hi // GROUP]),
                y_sb[:, 0 : hi - lo],
                wgo_sb[:, lo:hi],
                MULT,
            )
            if hi == S:
                nc.sync.dma_start(out[n * P : (n + 1) * P, :], pages[n % PAGES][:])

        up_tags = [None, "picked_0", "down_raw_0"]
        for i in range(PACK):
            gather(0, i, 0, S, picked_0[:, i, :])
        x_woven_0 = weave(nc.vector.tensor_copy, picked_0[:], "x_woven_0")
        up_raw.append(load_up(1, up_tags[1]))
        quantize(x_codes[0][:], x_sc[0][:], x_woven_0)
        down_woven_0 = weave_down(nc.scalar.copy, 0, 0, PACK)
        up_raw.append(load_up(2, up_tags[2]))
        quantize(down_codes[0][:], down_sc[0][:], down_woven_0)
        w4_rest = held([P, PASSES, 2 * (M - FIRST_COLS)], U8, "w4_rest", "down_woven_0_0")
        nc.sync.dma_start(w4_rest[:].bitcast(I32), w4_view[:, :, FIRST_COLS // 2 : M // 2])
        for q in range(4):
            h_passes(0, q)

        for i in range(2):
            gather(1, i, 0, HALF, picked_first[:, i, :])
            gather(1, i, HALF, S, picked_second[:, i, :])
        for copy, lo in ((nc.vector.tensor_copy, 0), (nc.scalar.copy, 2)):
            cols = slice(lo * P, (lo + 2) * P)
            quantize(down_codes[1][:, cols], down_sc[1][:, cols], weave_down(copy, 1, lo, lo + 2))

        gather(1, 2, 0, HALF, picked_first[:, 2, :])
        quarters = [slice(q * QUARTER, (q + 1) * QUARTER) for q in range(2)]
        for cols in quarters:
            gather(1, 3, cols.start, cols.stop, picked_first[:, 3, cols])
        x_woven_first = [
            weave(nc.vector.tensor_copy, picked_first[:, :, cols], "x_woven_first_%d" % q)
            for q, cols in enumerate(quarters)
        ]
        up_woven_0 = weave(nc.scalar.copy, up_raw[0][:], "up_woven_0")
        for q, cols in enumerate(quarters):
            quantize(x_codes[1][:, cols], x_sc[1][:, cols], x_woven_first[q])
            h_passes(1, q)
        h_woven_first = h_weave(0, "up_raw_0")
        bank_0_first = y_base(0, 0, HALF)

        gather(1, 2, HALF, S, picked_second[:, 2, :])
        gather(1, 3, HALF, S, picked_second[:, 3, :])
        quantize(up_codes[0][:], up_sc[0][:], up_woven_0)
        quantize(h_codes[:, 0:HALF], h_sc[:, 0:HALF], h_woven_first)
        x_woven_second = held([P, HALF, PACK], BF16, "x_woven_second", "up_raw_0")
        for cols in quarters:
            weave_into(nc.vector.tensor_copy, x_woven_second[:, cols, :], picked_second[:, :, cols])
        for q, cols in enumerate(quarters):
            tokens = slice(HALF + cols.start, HALF + cols.stop)
            quantize(x_codes[1][:, tokens], x_sc[1][:, tokens], x_woven_second[:, cols, :])
            h_passes(1, 2 + q)
        y_finish(0, 0, HALF, bank_0_first)
        h_woven_second = h_weave(1)
        quantize(h_codes[:, HALF:S], h_sc[:, HALF:S], h_woven_second)
        y_finish(1, 0, HALF, y_base(1, 0, HALF, psum_h.tile([P, S], F32, name="y_bank_1_first", tag="h_bank_2")))

        def up_chunk(c, width):
            quantize(up_codes[c][:], up_sc[c][:], weave(nc.scalar.copy, up_raw[c][:], "up_woven_%d" % c))
            return held([P, width], F32, "y_sb_after_up_%d" % c, up_tags[c])

        y_finish(0, HALF, S, y_base(0, HALF, S))
        y_finish(1, HALF, S, y_base(1, HALF, S), up_chunk(1, HALF))
        for n in range(SPLIT_TILES, M // P):
            y_sb = up_chunk(2, S) if n == LAST_CHUNK_BEFORE else None
            y_finish(n, 0, S, y_base(n, 0, S), y_sb)
